import numpy as np
import ml_dtypes


def mxq(x, axis, fmt="e4m3"):
    dtype, down = {"e4m3": (ml_dtypes.float8_e4m3fn, 7), "e5m2": (ml_dtypes.float8_e5m2, 14)}[fmt]
    v = np.moveaxis(np.asarray(x, np.float32).astype(ml_dtypes.bfloat16).astype(np.float64), axis, -1)
    blocks = v.reshape(v.shape[:-1] + (-1, 32))
    amax = np.abs(blocks).max(-1, keepdims=True)
    byte = np.maximum(np.where(amax > 0, np.frexp(amax)[1] - 1 + 127, 0) - down, 1)
    scale = np.exp2(byte - 127.0)
    codes = (blocks / scale).astype(np.float32).astype(dtype).astype(np.float64)
    return np.moveaxis((codes * scale).reshape(v.shape), -1, axis)


WIDE = False


def mx_kscale(k):
    if not WIDE:
        return np.ones(k)
    levels = np.array([10, -10, 5, -5, 0])
    if k % 512:
        return np.exp2(np.random.permutation(np.resize(levels, k // 32))).repeat(32)
    a = np.empty((k // 512, 16))
    for p in range(k // 512):
        a[p, :8] = np.random.permutation(np.resize(levels, 8))
        for g in range(8):
            far = levels[np.abs(levels - a[p, g]) >= 10]
            a[p, g + 8] = far[np.random.randint(len(far))]
    return np.exp2(a.ravel()).repeat(32)


def f64(x):
    return np.asarray(x).astype(np.float64)


def striped(idx):
    return np.tile(idx.reshape(-1, 16).T, (8, 1)).astype(np.uint16)


def unstriped(offs):
    return offs[:16].T.reshape(-1).astype(np.int64)


def pack_weight(w):
    k, n = w.shape
    w = f64(np.asarray(w, np.float32).astype(ml_dtypes.bfloat16)).reshape(k // 32, 32, n)
    amax = np.abs(w).max(1)
    byte = np.clip(np.where(amax > 0, np.frexp(amax)[1] - 1 + 127 - 7, 1), 1, 254)
    scaled = (w * np.exp2(127.0 - byte)[:, None, :]).reshape(k, n).astype(np.float32)
    words = np.ascontiguousarray(scaled.reshape(k // 512, 128, 4, n).transpose(0, 1, 3, 2)).astype(ml_dtypes.float8_e4m3fn).view(np.uint8)
    return words, np.ascontiguousarray(byte.astype(np.uint8).reshape(k // 512, 16, n))


def unpack_weight(words, scales):
    g, p, n, _ = words.shape
    vals = np.ascontiguousarray(words).view(ml_dtypes.float8_e4m3fn).astype(np.float64) * np.repeat(np.exp2(scales.astype(np.float64) - 127.0), 8, axis=1)[..., None]
    return vals.transpose(0, 1, 3, 2).reshape(g * 512, n)


K, T, S, N, R = 512, 1024, 512, 256, 256


def setup_inputs():
    n = np.random.standard_normal
    s = mx_kscale(K)[:, None]
    packed_xT = pack_weight(n((K, T)) * s)
    return {
        "x_words": packed_xT[0],
        "x_scales": packed_xT[1],
        "w1": (n((K, N)) / np.sqrt(K) / s).astype(np.float32),
        "slo": (np.random.uniform(0.5, 2.0, (N, R))).astype(np.float32),
        "icp": (n((N, R))).astype(np.float32),
        "lob": (-np.random.uniform(0.5, 1.5, (N, R))).astype(np.float32),
        "true": (n((N, S))).astype(np.float32),
        "offs": striped(np.random.permutation(T)[:S]),
        "seg": striped(np.random.permutation(np.concatenate([np.arange(R), np.random.randint(0, R, S - R)]))),
    }


def reference(x_words, x_scales, w1, slo, icp, lob, true, offs, seg):
    slog = f64(slo)[:, unstriped(seg)]
    xq = unpack_weight(x_words, x_scales)[:, unstriped(offs)]
    y = mxq(f64(w1), 0, "e4m3").T @ xq
    icpg = f64(icp)[:, unstriped(seg)]
    pos = slog * y + icpg
    lobg = f64(lob)[:, unstriped(seg)]
    pcl = np.maximum(pos, lobg)
    return np.log(np.abs(f64(true) - pcl) + 0.1)

@@ -1,0 +1,123 @@
+from contextlib import ExitStack
+
+import concourse.mybir as mybir
+
+K, T, S, N, R = 512, 1024, 512, 256, 256
+FLOPS = 2 * K * N * S
+
+F32 = mybir.dt.float32
+BF16 = mybir.dt.bfloat16
+I32 = mybir.dt.int32
+U32 = mybir.dt.uint32
+U16 = mybir.dt.uint16
+U8 = mybir.dt.uint8
+FP8X4 = mybir.dt.float8_e4m3fn_x4
+ALU = mybir.AluOpType
+ACT = mybir.ActivationFunctionType
+
+P = 128
+PACK = 4
+BLOCKS = N // P
+FUSED_WINDOW = S + 16
+COPY_WINDOW = 768
+
+
+def tile_picked_yrmidx_err_p_kernel(tc, x_words, x_scales, w1, slo, icp, lob, true, offs, seg, out):
+    nc = tc.nc
+    with ExitStack() as ctx:
+        keep = ctx.enter_context(tc.tile_pool(name="keep", bufs=1))
+        psum = ctx.enter_context(tc.psum_pool(name="psum", bufs=1))
+
+        seg_list = keep.tile([P, S // 16], U16, name="seg_list")
+        key_list = keep.tile([P, S // 16], U16, name="key_list")
+        all_words = keep.tile([P, T], I32, name="all_words", align_bytes=64)
+        all_scales = keep.tile([P, T], U8, name="all_scales", align_bytes=64)
+        w_raw = keep.tile([P, PACK, N], F32, name="w_raw", align_bytes=64)
+        lob_rows = keep.tile([P, R + COPY_WINDOW], F32, name="lob_rows", align_bytes=64)
+        slo_rows = [keep.tile([P, FUSED_WINDOW], F32, name="slo_rows%d" % b, align_bytes=64) for b in range(BLOCKS)]
+        icp_rows = [keep.tile([P, FUSED_WINDOW], F32, name="icp_rows%d" % b, align_bytes=64) for b in range(BLOCKS)]
+        true_rows = keep.tile([P, BLOCKS * S], F32, name="true_rows", align_bytes=64)
+
+        nc.vector.memset(all_scales[:].bitcast(I32), 0)
+        nc.vector.memset(lob_rows[:, BLOCKS * R :], 0.0)
+        for b in range(BLOCKS):
+            nc.gpsimd.memset(slo_rows[b][:, R:], 0.0)
+            nc.gpsimd.memset(icp_rows[b][:, R:], 0.0)
+
+        nc.sync.dma_start(seg_list[:], seg)
+        nc.sync.dma_start(
+            lob_rows[:, : BLOCKS * R].rearrange("p (b r) -> p b r", b=BLOCKS),
+            lob.rearrange("(b p) r -> p b r", p=P),
+        )
+        nc.sync.dma_start(key_list[:], offs)
+        for q in range(4):
+            nc.scalar.dma_start(
+                all_scales[32 * q : 32 * q + 4, :].bitcast(I32),
+                x_scales[0, 4 * q : 4 * q + 4, :].bitcast(I32),
+            )
+        nc.sync.dma_start(all_words[:], x_words[0].rearrange("p c t -> p (c t)").bitcast(I32))
+        nc.sync.dma_start(w_raw[:], w1.rearrange("(p j) n -> p j n", j=PACK))
+        for b in range(BLOCKS):
+            nc.sync.dma_start(slo_rows[b][:, :R], slo[b * P : (b + 1) * P, :])
+            nc.sync.dma_start(icp_rows[b][:, :R], icp[b * P : (b + 1) * P, :])
+        nc.sync.dma_start(
+            true_rows[:].rearrange("p (b s) -> p b s", b=BLOCKS),
+            true.rearrange("(b p) s -> p b s", p=P),
+        )
+
+        lob_g = [keep.tile([P, S], F32, name="lob_g%d" % b, align_bytes=64) for b in range(BLOCKS)]
+        key_words = keep.tile([P, S], U32, name="key_words", align_bytes=64)
+        key_scales = keep.tile([P, S], U8, name="key_scales", align_bytes=64)
+        w_codes = keep.tile([P, N], U32, name="w_codes", align_bytes=64)
+        w_scales = keep.tile([P, N], U8, name="w_scales", align_bytes=64)
+        w_grouped = keep.tile([P, N, PACK], BF16, name="w_grouped", align_bytes=64)
+
+        nc.scalar.copy(
+            w_grouped[:].rearrange("p (c i) t -> p c t i", i=4),
+            w_raw[:].rearrange("p t (c i) -> p c t i", i=4),
+        )
+        nc.vector.tensor_copy(lob_g[0][:], lob_rows[:, 0:COPY_WINDOW].indirect(seg_list[:]))
+        nc.vector.tensor_copy(key_scales[:], all_scales[:].indirect(key_list[:]))
+        nc.vector.tensor_copy(key_words[:], all_words[:].bitcast(U32).indirect(key_list[:]))
+        nc.vector.quantize_mx(
+            out=w_codes[:].bitcast(FP8X4), scales=w_scales[:], in_=w_grouped[:].rearrange("p n t -> p (n t)")
+        )
+        nc.vector.tensor_copy(lob_g[1][:], lob_rows[:, R : R + COPY_WINDOW].indirect(seg_list[:]))
+
+        y = []
+        for b in range(BLOCKS):
+            acc = psum.tile([P, S], F32, name="acc%d" % b)
+            cols = slice(b * P, (b + 1) * P)
+            nc.tensor.matmul_mx(
+                out=acc[:],
+                lhsT=w_codes[:, cols].bitcast(FP8X4),
+                lhsT_scale=w_scales[:, cols],
+                rhs=key_words[:].bitcast(FP8X4),
+                rhs_scale=key_scales[:],
+                start=True,
+                stop=True,
+            )
+            y_b = keep.tile([P, S], F32, name="y%d" % b, align_bytes=64)
+            nc.scalar.copy(y_b[:], acc[:])
+            y.append(y_b)
+
+        for b in range(BLOCKS):
+            scaled = keep.tile([P, S], F32, name="scaled%d" % b, align_bytes=64)
+            pos = keep.tile([P, S], F32, name="pos%d" % b, align_bytes=64)
+            nc.vector.tensor_tensor(scaled[:], slo_rows[b][:].indirect(seg_list[:]), y[b][:], ALU.mult)
+            nc.vector.tensor_tensor(pos[:], icp_rows[b][:].indirect(seg_list[:]), scaled[:], ALU.add)
+            pieces = 1 if b == 0 else 2
+            width = S // pieces
+            for h in range(pieces):
+                cols = slice(h * width, (h + 1) * width)
+                pcl = keep.tile([P, width], F32, name="pcl%d_%d" % (b, h), align_bytes=64)
+                diff = keep.tile([P, width], F32, name="diff%d_%d" % (b, h), align_bytes=64)
+                dist = keep.tile([P, width], F32, name="dist%d_%d" % (b, h), align_bytes=64)
+                res = keep.tile([P, width], F32, name="res%d_%d" % (b, h), align_bytes=64)
+                nc.vector.tensor_tensor(pcl[:], pos[:, cols], lob_g[b][:, cols], ALU.max)
+                nc.vector.tensor_tensor(
+                    diff[:], true_rows[:, b * S + h * width : b * S + (h + 1) * width], pcl[:], ALU.subtract
+                )
+                nc.scalar.activation(dist[:], diff[:], ACT.Abs)
+                nc.scalar.activation(res[:], dist[:], ACT.Ln, bias=0.1)
+                nc.sync.dma_start(out[b * P : (b + 1) * P, cols], res[:])

@@ -18,8 +18,9 @@ ACT = mybir.ActivationFunctionType
 P = 128
 PACK = 4
 BLOCKS = N // P
-FUSED_WINDOW = S + 16
-COPY_WINDOW = 768
+HALF = S // 2
+FUSED_WINDOW = HALF + 16
+COPY_WINDOW = 704
 
 
 def tile_picked_yrmidx_err_p_kernel(tc, x_words, x_scales, w1, slo, icp, lob, true, offs, seg, out):
@@ -28,96 +29,133 @@ def tile_picked_yrmidx_err_p_kernel(tc, x_words, x_scales, w1, slo, icp, lob, tr
         keep = ctx.enter_context(tc.tile_pool(name="keep", bufs=1))
         psum = ctx.enter_context(tc.psum_pool(name="psum", bufs=1))
 
+        def f32_tile(width, name):
+            return keep.tile([P, width], F32, name=name, align_bytes=64)
+
         seg_list = keep.tile([P, S // 16], U16, name="seg_list")
         key_list = keep.tile([P, S // 16], U16, name="key_list")
         all_words = keep.tile([P, T], I32, name="all_words", align_bytes=64)
         all_scales = keep.tile([P, T], U8, name="all_scales", align_bytes=64)
         w_raw = keep.tile([P, PACK, N], F32, name="w_raw", align_bytes=64)
-        lob_rows = keep.tile([P, R + COPY_WINDOW], F32, name="lob_rows", align_bytes=64)
-        slo_rows = [keep.tile([P, FUSED_WINDOW], F32, name="slo_rows%d" % b, align_bytes=64) for b in range(BLOCKS)]
-        icp_rows = [keep.tile([P, FUSED_WINDOW], F32, name="icp_rows%d" % b, align_bytes=64) for b in range(BLOCKS)]
-        true_rows = keep.tile([P, BLOCKS * S], F32, name="true_rows", align_bytes=64)
+        lob_rows = f32_tile(R + COPY_WINDOW, "lob_rows")
+        slo_rows = [f32_tile(FUSED_WINDOW, "slo_rows%d" % b) for b in range(BLOCKS)]
+        icp_rows = [f32_tile(FUSED_WINDOW, "icp_rows%d" % b) for b in range(BLOCKS)]
+        true_rows = [f32_tile(S, "true_rows%d" % b) for b in range(BLOCKS)]
+        one = f32_tile(1, "one")
+        warm = f32_tile(1, "warm")
 
-        nc.vector.memset(all_scales[:].bitcast(I32), 0)
+        nc.gpsimd.memset(all_scales[:].bitcast(I32), 0)
+        nc.gpsimd.memset(one[:], 1.0)
         nc.vector.memset(lob_rows[:, BLOCKS * R :], 0.0)
         for b in range(BLOCKS):
-            nc.gpsimd.memset(slo_rows[b][:, R:], 0.0)
-            nc.gpsimd.memset(icp_rows[b][:, R:], 0.0)
+            nc.vector.memset(slo_rows[b][:, R:], 0.0)
+            nc.vector.memset(icp_rows[b][:, R:], 0.0)
+
+        def rows(b):
+            return slice(b * P, (b + 1) * P)
+
+        def lob_start(b):
+            return (BLOCKS - 1 - b) * R
+
+        def load_lob(b):
+            nc.sync.dma_start(lob_rows[:, lob_start(b) : lob_start(b) + R], lob[rows(b), :])
 
         nc.sync.dma_start(seg_list[:], seg)
-        nc.sync.dma_start(
-            lob_rows[:, : BLOCKS * R].rearrange("p (b r) -> p b r", b=BLOCKS),
-            lob.rearrange("(b p) r -> p b r", p=P),
-        )
+        load_lob(0)
         nc.sync.dma_start(key_list[:], offs)
         for q in range(4):
             nc.scalar.dma_start(
                 all_scales[32 * q : 32 * q + 4, :].bitcast(I32),
                 x_scales[0, 4 * q : 4 * q + 4, :].bitcast(I32),
             )
-        nc.sync.dma_start(all_words[:], x_words[0].rearrange("p c t -> p (c t)").bitcast(I32))
+        nc.scalar.activation(warm[:], one[:], ACT.Ln)
         nc.sync.dma_start(w_raw[:], w1.rearrange("(p j) n -> p j n", j=PACK))
-        for b in range(BLOCKS):
-            nc.sync.dma_start(slo_rows[b][:, :R], slo[b * P : (b + 1) * P, :])
-            nc.sync.dma_start(icp_rows[b][:, :R], icp[b * P : (b + 1) * P, :])
-        nc.sync.dma_start(
-            true_rows[:].rearrange("p (b s) -> p b s", b=BLOCKS),
-            true.rearrange("(b p) s -> p b s", p=P),
-        )
+        nc.sync.dma_start(all_words[:], x_words[0].rearrange("p c t -> p (c t)").bitcast(I32))
+        nc.sync.dma_start(slo_rows[0][:, :R], slo[rows(0), :])
+        nc.sync.dma_start(icp_rows[0][:, :R], icp[rows(0), :])
+        load_lob(1)
+        nc.sync.dma_start(true_rows[0][:], true[rows(0), :])
+        nc.sync.dma_start(slo_rows[1][:, :R], slo[rows(1), :])
+        nc.sync.dma_start(icp_rows[1][:, :R], icp[rows(1), :])
+        nc.sync.dma_start(true_rows[1][:], true[rows(1), :])
 
-        lob_g = [keep.tile([P, S], F32, name="lob_g%d" % b, align_bytes=64) for b in range(BLOCKS)]
+        lob_g = [f32_tile(S, "lob_g%d" % b) for b in range(BLOCKS)]
         key_words = keep.tile([P, S], U32, name="key_words", align_bytes=64)
         key_scales = keep.tile([P, S], U8, name="key_scales", align_bytes=64)
         w_codes = keep.tile([P, N], U32, name="w_codes", align_bytes=64)
         w_scales = keep.tile([P, N], U8, name="w_scales", align_bytes=64)
         w_grouped = keep.tile([P, N, PACK], BF16, name="w_grouped", align_bytes=64)
 
+        def gather_lob(b):
+            window = lob_rows[:, lob_start(b) : lob_start(b) + COPY_WINDOW]
+            nc.vector.tensor_copy(lob_g[b][:], window.indirect(seg_list[:]))
+
         nc.scalar.copy(
             w_grouped[:].rearrange("p (c i) t -> p c t i", i=4),
             w_raw[:].rearrange("p t (c i) -> p c t i", i=4),
         )
-        nc.vector.tensor_copy(lob_g[0][:], lob_rows[:, 0:COPY_WINDOW].indirect(seg_list[:]))
+        gather_lob(0)
         nc.vector.tensor_copy(key_scales[:], all_scales[:].indirect(key_list[:]))
         nc.vector.tensor_copy(key_words[:], all_words[:].bitcast(U32).indirect(key_list[:]))
         nc.vector.quantize_mx(
             out=w_codes[:].bitcast(FP8X4), scales=w_scales[:], in_=w_grouped[:].rearrange("p n t -> p (n t)")
         )
-        nc.vector.tensor_copy(lob_g[1][:], lob_rows[:, R : R + COPY_WINDOW].indirect(seg_list[:]))
+        gather_lob(1)
+
+        pieces = [(b, h) for b in range(BLOCKS) for h in range(2)]
+
+        def cols(k):
+            return slice(pieces[k][1] * HALF, (pieces[k][1] + 1) * HALF)
+
+        def segs(k):
+            return seg_list[:, pieces[k][1] * HALF // 16 : (pieces[k][1] + 1) * HALF // 16]
 
         y = []
-        for b in range(BLOCKS):
-            acc = psum.tile([P, S], F32, name="acc%d" % b)
-            cols = slice(b * P, (b + 1) * P)
+        for k in range(len(pieces)):
+            b = pieces[k][0]
+            acc = psum.tile([P, HALF], F32, name="acc%d" % k)
             nc.tensor.matmul_mx(
                 out=acc[:],
-                lhsT=w_codes[:, cols].bitcast(FP8X4),
-                lhsT_scale=w_scales[:, cols],
-                rhs=key_words[:].bitcast(FP8X4),
-                rhs_scale=key_scales[:],
+                lhsT=w_codes[:, rows(b)].bitcast(FP8X4),
+                lhsT_scale=w_scales[:, rows(b)],
+                rhs=key_words[:, cols(k)].bitcast(FP8X4),
+                rhs_scale=key_scales[:, cols(k)],
                 start=True,
                 stop=True,
             )
-            y_b = keep.tile([P, S], F32, name="y%d" % b, align_bytes=64)
-            nc.scalar.copy(y_b[:], acc[:])
-            y.append(y_b)
+            y.append(f32_tile(HALF, "y%d" % k))
+            nc.scalar.copy(y[k][:], acc[:])
 
-        for b in range(BLOCKS):
-            scaled = keep.tile([P, S], F32, name="scaled%d" % b, align_bytes=64)
-            pos = keep.tile([P, S], F32, name="pos%d" % b, align_bytes=64)
-            nc.vector.tensor_tensor(scaled[:], slo_rows[b][:].indirect(seg_list[:]), y[b][:], ALU.mult)
-            nc.vector.tensor_tensor(pos[:], icp_rows[b][:].indirect(seg_list[:]), scaled[:], ALU.add)
-            pieces = 1 if b == 0 else 2
-            width = S // pieces
-            for h in range(pieces):
-                cols = slice(h * width, (h + 1) * width)
-                pcl = keep.tile([P, width], F32, name="pcl%d_%d" % (b, h), align_bytes=64)
-                diff = keep.tile([P, width], F32, name="diff%d_%d" % (b, h), align_bytes=64)
-                dist = keep.tile([P, width], F32, name="dist%d_%d" % (b, h), align_bytes=64)
-                res = keep.tile([P, width], F32, name="res%d_%d" % (b, h), align_bytes=64)
-                nc.vector.tensor_tensor(pcl[:], pos[:, cols], lob_g[b][:, cols], ALU.max)
-                nc.vector.tensor_tensor(
-                    diff[:], true_rows[:, b * S + h * width : b * S + (h + 1) * width], pcl[:], ALU.subtract
-                )
-                nc.scalar.activation(dist[:], diff[:], ACT.Abs)
-                nc.scalar.activation(res[:], dist[:], ACT.Ln, bias=0.1)
-                nc.sync.dma_start(out[b * P : (b + 1) * P, cols], res[:])
+        scaled = [f32_tile(HALF, "scaled%d" % k) for k in range(len(pieces))]
+        pos = [f32_tile(HALF, "pos%d" % k) for k in range(len(pieces))]
+        pcl = [f32_tile(HALF, "pcl%d" % k) for k in range(len(pieces))]
+
+        def slope(k):
+            nc.vector.tensor_tensor(scaled[k][:], slo_rows[pieces[k][0]][:].indirect(segs(k)), y[k][:], ALU.mult)
+
+        def intercept(k):
+            nc.vector.tensor_tensor(pos[k][:], icp_rows[pieces[k][0]][:].indirect(segs(k)), scaled[k][:], ALU.add)
+
+        def bound(k):
+            nc.vector.tensor_tensor(pcl[k][:], pos[k][:], lob_g[pieces[k][0]][:, cols(k)], ALU.max)
+
+        def finish(k):
+            b = pieces[k][0]
+            diff = f32_tile(HALF, "diff%d" % k)
+            dist = f32_tile(HALF, "dist%d" % k)
+            res = f32_tile(HALF, "res%d" % k)
+            nc.vector.tensor_tensor(diff[:], true_rows[b][:, cols(k)], pcl[k][:], ALU.subtract)
+            nc.scalar.activation(dist[:], diff[:], ACT.Abs)
+            nc.scalar.activation(res[:], dist[:], ACT.Ln, bias=0.1)
+            nc.sync.dma_start(out[rows(b), cols(k)], res[:])
+
+        slope(0)
+        slope(1)
+        intercept(0)
+        for k in range(len(pieces)):
+            if k + 2 < len(pieces):
+                slope(k + 2)
+            bound(k)
+            if k + 1 < len(pieces):
+                intercept(k + 1)
+            finish(k)

@@ -38,30 +38,43 @@ def tile_picked_yrmidx_err_p_kernel(tc, x_words, x_scales, w1, slo, icp, lob, tr
         all_scales = keep.tile([P, T], U8, name="all_scales", align_bytes=64)
         w_raw = keep.tile([P, PACK, N], F32, name="w_raw", align_bytes=64)
         lob_rows = f32_tile(R + COPY_WINDOW, "lob_rows")
+        icp_rows = f32_tile(R + COPY_WINDOW, "icp_rows")
         slo_rows = [f32_tile(FUSED_WINDOW, "slo_rows%d" % b) for b in range(BLOCKS)]
-        icp_rows = [f32_tile(FUSED_WINDOW, "icp_rows%d" % b) for b in range(BLOCKS)]
         true_rows = [f32_tile(S, "true_rows%d" % b) for b in range(BLOCKS)]
-        one = f32_tile(1, "one")
         warm = f32_tile(1, "warm")
+        identity = f32_tile(P, "identity")
 
         nc.gpsimd.memset(all_scales[:].bitcast(I32), 0)
+        one = f32_tile(1, "one")
         nc.gpsimd.memset(one[:], 1.0)
+        ones = f32_tile(32, "ones")
+        column = f32_tile(32, "column")
+        lane = f32_tile(32, "lane")
+        nc.vector.memset(ones[:], 1.0)
+        nc.vector.memset(identity[:], 0.0)
+        nc.vector.tensor_tensor_scan(column[:], ones[:], ones[:], 0.0, ALU.mult, ALU.add)
+        nc.vector.transpose(lane[:], column[:])
+        for q in range(0, P, 32):
+            nc.vector.tensor_tensor(
+                identity[q : q + 32, q : q + 32], column[q : q + 32, :], lane[q : q + 32, :], ALU.is_equal
+            )
         nc.vector.memset(lob_rows[:, BLOCKS * R :], 0.0)
+        nc.gpsimd.memset(icp_rows[:, BLOCKS * R :], 0.0)
         for b in range(BLOCKS):
             nc.vector.memset(slo_rows[b][:, R:], 0.0)
-            nc.vector.memset(icp_rows[b][:, R:], 0.0)
 
         def rows(b):
             return slice(b * P, (b + 1) * P)
 
-        def lob_start(b):
+        def table_start(b):
             return (BLOCKS - 1 - b) * R
 
-        def load_lob(b):
-            nc.sync.dma_start(lob_rows[:, lob_start(b) : lob_start(b) + R], lob[rows(b), :])
+        def load_table(tile, table, b):
+            nc.sync.dma_start(tile[:, table_start(b) : table_start(b) + R], table[rows(b), :])
 
         nc.sync.dma_start(seg_list[:], seg)
-        load_lob(0)
+        load_table(lob_rows, lob, 0)
+        load_table(icp_rows, icp, 0)
         nc.sync.dma_start(key_list[:], offs)
         for q in range(4):
             nc.scalar.dma_start(
@@ -71,91 +84,109 @@ def tile_picked_yrmidx_err_p_kernel(tc, x_words, x_scales, w1, slo, icp, lob, tr
         nc.scalar.activation(warm[:], one[:], ACT.Ln)
         nc.sync.dma_start(w_raw[:], w1.rearrange("(p j) n -> p j n", j=PACK))
         nc.sync.dma_start(all_words[:], x_words[0].rearrange("p c t -> p (c t)").bitcast(I32))
-        nc.sync.dma_start(slo_rows[0][:, :R], slo[rows(0), :])
-        nc.sync.dma_start(icp_rows[0][:, :R], icp[rows(0), :])
-        load_lob(1)
         nc.sync.dma_start(true_rows[0][:], true[rows(0), :])
-        nc.sync.dma_start(slo_rows[1][:, :R], slo[rows(1), :])
-        nc.sync.dma_start(icp_rows[1][:, :R], icp[rows(1), :])
+        load_table(lob_rows, lob, 1)
+        load_table(icp_rows, icp, 1)
+        nc.sync.dma_start(slo_rows[0][:, :R], slo[rows(0), :])
         nc.sync.dma_start(true_rows[1][:], true[rows(1), :])
+        nc.sync.dma_start(slo_rows[1][:, :R], slo[rows(1), :])
 
         lob_g = [f32_tile(S, "lob_g%d" % b) for b in range(BLOCKS)]
+        icp_g = [f32_tile(S, "icp_g%d" % b) for b in range(BLOCKS)]
+        minus_true = [f32_tile(S, "minus_true%d" % b) for b in range(BLOCKS)]
         key_words = keep.tile([P, S], U32, name="key_words", align_bytes=64)
         key_scales = keep.tile([P, S], U8, name="key_scales", align_bytes=64)
         w_codes = keep.tile([P, N], U32, name="w_codes", align_bytes=64)
         w_scales = keep.tile([P, N], U8, name="w_scales", align_bytes=64)
         w_grouped = keep.tile([P, N, PACK], BF16, name="w_grouped", align_bytes=64)
 
-        def gather_lob(b):
-            window = lob_rows[:, lob_start(b) : lob_start(b) + COPY_WINDOW]
-            nc.vector.tensor_copy(lob_g[b][:], window.indirect(seg_list[:]))
+        def gather_table(picked, tile, b):
+            window = tile[:, table_start(b) : table_start(b) + COPY_WINDOW]
+            nc.vector.tensor_copy(picked[b][:], window.indirect(seg_list[:]))
 
         nc.scalar.copy(
             w_grouped[:].rearrange("p (c i) t -> p c t i", i=4),
             w_raw[:].rearrange("p t (c i) -> p c t i", i=4),
         )
-        gather_lob(0)
+        gather_table(lob_g, lob_rows, 0)
+        gather_table(icp_g, icp_rows, 0)
         nc.vector.tensor_copy(key_scales[:], all_scales[:].indirect(key_list[:]))
         nc.vector.tensor_copy(key_words[:], all_words[:].bitcast(U32).indirect(key_list[:]))
         nc.vector.quantize_mx(
             out=w_codes[:].bitcast(FP8X4), scales=w_scales[:], in_=w_grouped[:].rearrange("p n t -> p (n t)")
         )
-        gather_lob(1)
+        gather_table(lob_g, lob_rows, 1)
+        gather_table(icp_g, icp_rows, 1)
 
-        pieces = [(b, h) for b in range(BLOCKS) for h in range(2)]
+        pieces = [(0, 0, 256), (0, 256, 256), (1, 0, 256), (1, 256, 128), (1, 384, 128)]
 
-        def cols(k):
-            return slice(pieces[k][1] * HALF, (pieces[k][1] + 1) * HALF)
+        def add_turned(bank, term, first=False, last=False):
+            width = term.shape[1]
+            for c in range(0, width, P):
+                nc.tensor.matmul(
+                    bank[:, c : c + P],
+                    lhsT=term[:, c : c + P],
+                    rhs=identity[:],
+                    is_transpose=True,
+                    start=(first and c == 0),
+                    stop=(last and c + P == width),
+                )
 
-        def segs(k):
-            return seg_list[:, pieces[k][1] * HALF // 16 : (pieces[k][1] + 1) * HALF // 16]
+        y = [f32_tile(S, "y%d" % b) for b in range(BLOCKS)]
+        floor_t = [f32_tile(S, "floor_t%d" % b) for b in range(BLOCKS)]
+        banks = {}
 
-        y = []
-        for k in range(len(pieces)):
-            b = pieces[k][0]
-            acc = psum.tile([P, HALF], F32, name="acc%d" % k)
+        def open_sums(b):
+            mine = [k for k in range(len(pieces)) if pieces[k][0] == b]
+            nc.scalar.activation(minus_true[b][:], true_rows[b][:], ACT.Copy, scale=-1.0)
+            floor_bank = psum.tile([P, S], F32, name="floor_bank%d" % b, tag="floor")
+            add_turned(floor_bank, lob_g[b][:], first=True)
+            for k in mine:
+                j, width = pieces[k][1:]
+                banks[k] = psum.tile([P, width], F32, name="pos_bank%d" % k, tag="pos%d" % k)
+                add_turned(banks[k], icp_g[b][:, j : j + width], first=True)
+            add_turned(floor_bank, minus_true[b][:], last=True)
+            for k in mine:
+                j, width = pieces[k][1:]
+                add_turned(banks[k], minus_true[b][:, j : j + width])
+            nc.scalar.copy(floor_t[b][:], floor_bank[:])
+
+        open_sums(0)
+        for b in range(BLOCKS):
+            acc = psum.tile([P, S], F32, name="acc%d" % b, tag="acc%d" % b)
             nc.tensor.matmul_mx(
                 out=acc[:],
                 lhsT=w_codes[:, rows(b)].bitcast(FP8X4),
                 lhsT_scale=w_scales[:, rows(b)],
-                rhs=key_words[:, cols(k)].bitcast(FP8X4),
-                rhs_scale=key_scales[:, cols(k)],
+                rhs=key_words[:].bitcast(FP8X4),
+                rhs_scale=key_scales[:],
                 start=True,
                 stop=True,
             )
-            y.append(f32_tile(HALF, "y%d" % k))
-            nc.scalar.copy(y[k][:], acc[:])
-
-        scaled = [f32_tile(HALF, "scaled%d" % k) for k in range(len(pieces))]
-        pos = [f32_tile(HALF, "pos%d" % k) for k in range(len(pieces))]
-        pcl = [f32_tile(HALF, "pcl%d" % k) for k in range(len(pieces))]
+            nc.scalar.copy(y[b][:], acc[:])
+        open_sums(1)
 
         def slope(k):
-            nc.vector.tensor_tensor(scaled[k][:], slo_rows[pieces[k][0]][:].indirect(segs(k)), y[k][:], ALU.mult)
-
-        def intercept(k):
-            nc.vector.tensor_tensor(pos[k][:], icp_rows[pieces[k][0]][:].indirect(segs(k)), scaled[k][:], ALU.add)
-
-        def bound(k):
-            nc.vector.tensor_tensor(pcl[k][:], pos[k][:], lob_g[pieces[k][0]][:, cols(k)], ALU.max)
+            b, j, width = pieces[k]
+            scaled = f32_tile(width, "scaled%d" % k)
+            segs = seg_list[:, j // 16 : (j + width) // 16]
+            nc.vector.tensor_tensor(scaled[:], slo_rows[b][:].indirect(segs), y[b][:, j : j + width], ALU.mult)
+            add_turned(banks[k], scaled[:], last=True)
 
         def finish(k):
-            b = pieces[k][0]
-            diff = f32_tile(HALF, "diff%d" % k)
-            dist = f32_tile(HALF, "dist%d" % k)
-            res = f32_tile(HALF, "res%d" % k)
-            nc.vector.tensor_tensor(diff[:], true_rows[b][:, cols(k)], pcl[k][:], ALU.subtract)
-            nc.scalar.activation(dist[:], diff[:], ACT.Abs)
+            b, j, width = pieces[k]
+            diff_t = f32_tile(width, "diff_t%d" % k)
+            dist = f32_tile(width, "dist%d" % k)
+            res = f32_tile(width, "res%d" % k)
+            nc.vector.tensor_tensor(diff_t[:], banks[k][:], floor_t[b][:, j : j + width], ALU.max)
+            back = psum.tile([P, width], F32, name="back%d" % k, tag=("acc0", "acc1", "floor")[k % 3])
+            add_turned(back, diff_t[:], first=True, last=True)
+            nc.scalar.activation(dist[:], back[:], ACT.Abs)
             nc.scalar.activation(res[:], dist[:], ACT.Ln, bias=0.1)
-            nc.sync.dma_start(out[rows(b), cols(k)], res[:])
+            nc.sync.dma_start(out[rows(b), j : j + width], res[:])
 
         slope(0)
-        slope(1)
-        intercept(0)
         for k in range(len(pieces)):
-            if k + 2 < len(pieces):
-                slope(k + 2)
-            bound(k)
             if k + 1 < len(pieces):
-                intercept(k + 1)
+                slope(k + 1)
             finish(k)

from contextlib import ExitStack

import concourse.mybir as mybir

K, T, S, N, R = 512, 1024, 512, 256, 256
FLOPS = 2 * K * N * S

F32 = mybir.dt.float32
BF16 = mybir.dt.bfloat16
I32 = mybir.dt.int32
U32 = mybir.dt.uint32
U16 = mybir.dt.uint16
U8 = mybir.dt.uint8
FP8X4 = mybir.dt.float8_e4m3fn_x4
ALU = mybir.AluOpType
ACT = mybir.ActivationFunctionType

P = 128
PACK = 4
BLOCKS = N // P
HALF = S // 2
FUSED_WINDOW = HALF + 16
COPY_WINDOW = 704


def tile_picked_yrmidx_err_p_kernel(tc, x_words, x_scales, w1, slo, icp, lob, true, offs, seg, out):
    nc = tc.nc
    with ExitStack() as ctx:
        keep = ctx.enter_context(tc.tile_pool(name="keep", bufs=1))
        psum = ctx.enter_context(tc.psum_pool(name="psum", bufs=1))

        def f32_tile(width, name):
            return keep.tile([P, width], F32, name=name, align_bytes=64)

        seg_list = keep.tile([P, S // 16], U16, name="seg_list")
        key_list = keep.tile([P, S // 16], U16, name="key_list")
        all_words = keep.tile([P, T], I32, name="all_words", align_bytes=64)
        all_scales = keep.tile([P, T], U8, name="all_scales", align_bytes=64)
        w_raw = keep.tile([P, PACK, N], F32, name="w_raw", align_bytes=64)
        lob_rows = f32_tile(R + COPY_WINDOW, "lob_rows")
        icp_rows = f32_tile(R + COPY_WINDOW, "icp_rows")
        slo_rows = [f32_tile(FUSED_WINDOW, "slo_rows%d" % b) for b in range(BLOCKS)]
        true_rows = [f32_tile(S, "true_rows%d" % b) for b in range(BLOCKS)]
        warm = f32_tile(1, "warm")
        identity = f32_tile(P, "identity")

        nc.gpsimd.memset(all_scales[:].bitcast(I32), 0)
        one = f32_tile(1, "one")
        nc.gpsimd.memset(one[:], 1.0)
        ones = f32_tile(32, "ones")
        column = f32_tile(32, "column")
        lane = f32_tile(32, "lane")
        nc.vector.memset(ones[:], 1.0)
        nc.vector.memset(identity[:], 0.0)
        nc.vector.tensor_tensor_scan(column[:], ones[:], ones[:], 0.0, ALU.mult, ALU.add)
        nc.vector.transpose(lane[:], column[:])
        for q in range(0, P, 32):
            nc.vector.tensor_tensor(
                identity[q : q + 32, q : q + 32], column[q : q + 32, :], lane[q : q + 32, :], ALU.is_equal
            )
        nc.vector.memset(lob_rows[:, BLOCKS * R :], 0.0)
        nc.gpsimd.memset(icp_rows[:, BLOCKS * R :], 0.0)
        for b in range(BLOCKS):
            nc.vector.memset(slo_rows[b][:, R:], 0.0)

        def rows(b):
            return slice(b * P, (b + 1) * P)

        def table_start(b):
            return (BLOCKS - 1 - b) * R

        def load_table(tile, table, b):
            nc.sync.dma_start(tile[:, table_start(b) : table_start(b) + R], table[rows(b), :])

        nc.sync.dma_start(seg_list[:], seg)
        load_table(lob_rows, lob, 0)
        load_table(icp_rows, icp, 0)
        nc.sync.dma_start(key_list[:], offs)
        for q in range(4):
            nc.scalar.dma_start(
                all_scales[32 * q : 32 * q + 4, :].bitcast(I32),
                x_scales[0, 4 * q : 4 * q + 4, :].bitcast(I32),
            )
        nc.scalar.activation(warm[:], one[:], ACT.Ln)
        nc.sync.dma_start(w_raw[:], w1.rearrange("(p j) n -> p j n", j=PACK))
        nc.sync.dma_start(all_words[:], x_words[0].rearrange("p c t -> p (c t)").bitcast(I32))
        nc.sync.dma_start(true_rows[0][:], true[rows(0), :])
        load_table(lob_rows, lob, 1)
        load_table(icp_rows, icp, 1)
        nc.sync.dma_start(slo_rows[0][:, :R], slo[rows(0), :])
        nc.sync.dma_start(true_rows[1][:], true[rows(1), :])
        nc.sync.dma_start(slo_rows[1][:, :R], slo[rows(1), :])

        lob_g = [f32_tile(S, "lob_g%d" % b) for b in range(BLOCKS)]
        icp_g = [f32_tile(S, "icp_g%d" % b) for b in range(BLOCKS)]
        minus_true = [f32_tile(S, "minus_true%d" % b) for b in range(BLOCKS)]
        key_words = keep.tile([P, S], U32, name="key_words", align_bytes=64)
        key_scales = keep.tile([P, S], U8, name="key_scales", align_bytes=64)
        w_codes = keep.tile([P, N], U32, name="w_codes", align_bytes=64)
        w_scales = keep.tile([P, N], U8, name="w_scales", align_bytes=64)
        w_grouped = keep.tile([P, N, PACK], BF16, name="w_grouped", align_bytes=64)

        def gather_table(picked, tile, b):
            window = tile[:, table_start(b) : table_start(b) + COPY_WINDOW]
            nc.vector.tensor_copy(picked[b][:], window.indirect(seg_list[:]))

        nc.scalar.copy(
            w_grouped[:].rearrange("p (c i) t -> p c t i", i=4),
            w_raw[:].rearrange("p t (c i) -> p c t i", i=4),
        )
        gather_table(lob_g, lob_rows, 0)
        gather_table(icp_g, icp_rows, 0)
        nc.vector.tensor_copy(key_scales[:], all_scales[:].indirect(key_list[:]))
        nc.vector.tensor_copy(key_words[:], all_words[:].bitcast(U32).indirect(key_list[:]))
        nc.vector.quantize_mx(
            out=w_codes[:].bitcast(FP8X4), scales=w_scales[:], in_=w_grouped[:].rearrange("p n t -> p (n t)")
        )
        gather_table(lob_g, lob_rows, 1)
        gather_table(icp_g, icp_rows, 1)

        pieces = [(0, 0, 256), (0, 256, 256), (1, 0, 256), (1, 256, 128), (1, 384, 128)]

        def add_turned(bank, term, first=False, last=False):
            width = term.shape[1]
            for c in range(0, width, P):
                nc.tensor.matmul(
                    bank[:, c : c + P],
                    lhsT=term[:, c : c + P],
                    rhs=identity[:],
                    is_transpose=True,
                    start=(first and c == 0),
                    stop=(last and c + P == width),
                )

        y = [f32_tile(S, "y%d" % b) for b in range(BLOCKS)]
        floor_t = [f32_tile(S, "floor_t%d" % b) for b in range(BLOCKS)]
        banks = {}

        def open_sums(b):
            mine = [k for k in range(len(pieces)) if pieces[k][0] == b]
            nc.scalar.activation(minus_true[b][:], true_rows[b][:], ACT.Copy, scale=-1.0)
            floor_bank = psum.tile([P, S], F32, name="floor_bank%d" % b, tag="floor")
            add_turned(floor_bank, lob_g[b][:], first=True)
            for k in mine:
                j, width = pieces[k][1:]
                banks[k] = psum.tile([P, width], F32, name="pos_bank%d" % k, tag="pos%d" % k)
                add_turned(banks[k], icp_g[b][:, j : j + width], first=True)
            add_turned(floor_bank, minus_true[b][:], last=True)
            for k in mine:
                j, width = pieces[k][1:]
                add_turned(banks[k], minus_true[b][:, j : j + width])
            nc.scalar.copy(floor_t[b][:], floor_bank[:])

        open_sums(0)
        for b in range(BLOCKS):
            acc = psum.tile([P, S], F32, name="acc%d" % b, tag="acc%d" % b)
            nc.tensor.matmul_mx(
                out=acc[:],
                lhsT=w_codes[:, rows(b)].bitcast(FP8X4),
                lhsT_scale=w_scales[:, rows(b)],
                rhs=key_words[:].bitcast(FP8X4),
                rhs_scale=key_scales[:],
                start=True,
                stop=True,
            )
            nc.scalar.copy(y[b][:], acc[:])
        open_sums(1)

        def slope(k):
            b, j, width = pieces[k]
            scaled = f32_tile(width, "scaled%d" % k)
            segs = seg_list[:, j // 16 : (j + width) // 16]
            nc.vector.tensor_tensor(scaled[:], slo_rows[b][:].indirect(segs), y[b][:, j : j + width], ALU.mult)
            add_turned(banks[k], scaled[:], last=True)

        def finish(k):
            b, j, width = pieces[k]
            diff_t = f32_tile(width, "diff_t%d" % k)
            dist = f32_tile(width, "dist%d" % k)
            res = f32_tile(width, "res%d" % k)
            nc.vector.tensor_tensor(diff_t[:], banks[k][:], floor_t[b][:, j : j + width], ALU.max)
            back = psum.tile([P, width], F32, name="back%d" % k, tag=("acc0", "acc1", "floor")[k % 3])
            add_turned(back, diff_t[:], first=True, last=True)
            nc.scalar.activation(dist[:], back[:], ACT.Abs)
            nc.scalar.activation(res[:], dist[:], ACT.Ln, bias=0.1)
            nc.sync.dma_start(out[rows(b), j : j + width], res[:])

        slope(0)
        for k in range(len(pieces)):
            if k + 1 < len(pieces):
                slope(k + 1)
            finish(k)
